import numpy as np
import ml_dtypes


def mxq(x, axis, fmt="e4m3"):
    dtype, down = {"e4m3": (ml_dtypes.float8_e4m3fn, 7), "e5m2": (ml_dtypes.float8_e5m2, 14)}[fmt]
    v = np.moveaxis(np.asarray(x, np.float32).astype(ml_dtypes.bfloat16).astype(np.float64), axis, -1)
    blocks = v.reshape(v.shape[:-1] + (-1, 32))
    amax = np.abs(blocks).max(-1, keepdims=True)
    byte = np.maximum(np.where(amax > 0, np.frexp(amax)[1] - 1 + 127, 0) - down, 1)
    scale = np.exp2(byte - 127.0)
    codes = (blocks / scale).astype(np.float32).astype(dtype).astype(np.float64)
    return np.moveaxis((codes * scale).reshape(v.shape), -1, axis)


WIDE = False


def mx_kscale(k):
    if not WIDE:
        return np.ones(k)
    levels = np.array([10, -10, 5, -5, 0])
    if k % 512:
        return np.exp2(np.random.permutation(np.resize(levels, k // 32))).repeat(32)
    a = np.empty((k // 512, 16))
    for p in range(k // 512):
        a[p, :8] = np.random.permutation(np.resize(levels, 8))
        for g in range(8):
            far = levels[np.abs(levels - a[p, g]) >= 10]
            a[p, g + 8] = far[np.random.randint(len(far))]
    return np.exp2(a.ravel()).repeat(32)


def f64(x):
    return np.asarray(x).astype(np.float64)


def striped(idx):
    return np.tile(idx.reshape(-1, 16).T, (8, 1)).astype(np.uint16)


def unstriped(offs):
    return offs[:16].T.reshape(-1).astype(np.int64)


def striped8(idx):
    return np.concatenate([x.reshape(-1, 16).T for x in idx]).astype(np.uint16)


def runs(offs, k):
    lists = np.stack([offs[16 * r : 16 * r + 16].T.reshape(-1) for r in range(8)]).astype(np.int64)
    return lists[np.arange(k) % 512 // 64]


def pack_weight(w):
    k, n = w.shape
    w = f64(np.asarray(w, np.float32).astype(ml_dtypes.bfloat16)).reshape(k // 32, 32, n)
    amax = np.abs(w).max(1)
    byte = np.clip(np.where(amax > 0, np.frexp(amax)[1] - 1 + 127 - 7, 1), 1, 254)
    scaled = (w * np.exp2(127.0 - byte)[:, None, :]).reshape(k, n).astype(np.float32)
    words = np.ascontiguousarray(scaled.reshape(k // 512, 128, 4, n).transpose(0, 1, 3, 2)).astype(ml_dtypes.float8_e4m3fn).view(np.uint8)
    return words, np.ascontiguousarray(byte.astype(np.uint8).reshape(k // 512, 16, n))


def unpack_weight(words, scales):
    g, p, n, _ = words.shape
    vals = np.ascontiguousarray(words).view(ml_dtypes.float8_e4m3fn).astype(np.float64) * np.repeat(np.exp2(scales.astype(np.float64) - 127.0), 8, axis=1)[..., None]
    return vals.transpose(0, 1, 3, 2).reshape(g * 512, n)


E2M1 = np.array([0.0, 0.5, 1.0, 1.5, 2.0, 3.0, 4.0, 6.0, -0.0, -0.5, -1.0, -1.5, -2.0, -3.0, -4.0, -6.0])


def pack_fp4(w):
    k, n = w.shape
    w = f64(np.asarray(w, np.float32).astype(ml_dtypes.bfloat16)).reshape(k // 32, 32, n)
    amax = np.abs(w).max(1)
    mant, ex = np.frexp(amax / 6.0)
    byte = np.clip(np.where(amax > 0, np.where(mant > 0.5, ex, ex - 1) + 127, 1), 1, 254)
    scaled = (w * np.exp2(127.0 - byte)[:, None, :]).reshape(k, n).astype(np.float32)
    c = np.ascontiguousarray(scaled.reshape(k // 512, 128, 4, n).transpose(0, 1, 3, 2)).astype(ml_dtypes.float4_e2m1fn).view(np.uint8) & 0xF
    words = (c[..., 0::2] | (c[..., 1::2] << 4)).reshape(k // 512, 128, 2 * n)
    return np.ascontiguousarray(words), np.ascontiguousarray(byte.astype(np.uint8).reshape(k // 512, 16, n))


def unpack_fp4(words, scales):
    g, _, n = scales.shape
    words = np.ascontiguousarray(words).reshape(g, 128, n, 2)
    nib = np.empty((g, 128, n, 4), np.uint8)
    nib[..., 0::2] = words & 0xF
    nib[..., 1::2] = words >> 4
    vals = E2M1[nib] * np.repeat(np.exp2(scales.astype(np.float64) - 127.0), 8, axis=1)[..., None]
    return vals.transpose(0, 1, 3, 2).reshape(g * 512, n)


def planes(y):
    n, m = y.shape
    v = y.astype(np.float32).astype(ml_dtypes.bfloat16).astype(np.float64).reshape(n // 32, 32, m)
    top = np.abs(v).max(1)
    byte = np.clip(np.where(top > 0, np.frexp(top)[1] - 1 + 127 - 7, 1), 1, 254)
    codes = (v * np.exp2(127.0 - byte)[:, None, :]).reshape(n, m).astype(np.float32).astype(ml_dtypes.float8_e4m3fn).view(np.uint8)
    words = codes.reshape(n // 512, 128, 4, m).transpose(0, 1, 3, 2)
    return np.ascontiguousarray(words), np.ascontiguousarray(byte.astype(np.uint8).reshape(n // 512, 16, m))


K, T, S, V, H = 512, 2048, 512, 512, 512


def setup_inputs():
    n = np.random.standard_normal
    s = mx_kscale(K)[:, None]
    packed_xT = pack_weight(n((K, T)) * s)
    packed_w1 = pack_fp4(n((K, H)) / np.sqrt(K) / s)
    return {
        "x_words": packed_xT[0],
        "x_scales": packed_xT[1],
        "w1_words": packed_w1[0],
        "w1_scales": packed_w1[1],
        "gs": (np.random.uniform(0.5, 1.5, (K, 1)) / s).astype(np.float32),
        "offs": striped(np.random.permutation(T)[:S]),
        "nb": striped8(np.stack([np.random.permutation(S) for _ in range(8)])),
        "cand": striped(np.random.permutation(T)[:V]),
    }


def reference(x_words, x_scales, w1_words, w1_scales, gs, offs, nb, cand):
    x_cand = unpack_weight(x_words, x_scales)[:, unstriped(cand)]
    xq = unpack_weight(x_words, x_scales)[:, unstriped(offs)]
    h = unpack_fp4(w1_words, w1_scales).T @ xq
    z = f64(gs) * (h * (h[np.arange(H)[:, None], runs(nb, H)]))
    out_0 = 0.0625 * ((x_cand.T @ mxq(z, 0, "e4m3")))
    return (out_0,) + planes(out_0)

@@ -1,0 +1,186 @@
+from contextlib import ExitStack
+
+import concourse.mybir as mybir
+
+F32 = mybir.dt.float32
+BF16 = mybir.dt.bfloat16
+I32 = mybir.dt.int32
+U32 = mybir.dt.uint32
+U16 = mybir.dt.uint16
+U8 = mybir.dt.uint8
+FP8X4 = mybir.dt.float8_e4m3fn_x4
+FP4X4 = mybir.dt.float4_e2m1fn_x4
+COPY = mybir.ActivationFunctionType.Copy
+MULT = mybir.AluOpType.mult
+
+P = 128
+T = 2048
+S = 512
+PACK = 4
+CH = 128
+NCH = S // CH
+HALF = 256
+FLOPS = 2 * 2 * 512 * 512 * 512
+
+
+def tile_picked_candbil_none_po_kernel(
+    tc, x_words, x_scales, w1_words, w1_scales, gs, offs, nb, cand, out_0, out_1, out_2
+):
+    nc = tc.nc
+    with ExitStack() as ctx:
+        keep = ctx.enter_context(tc.tile_pool(name="keep", bufs=1))
+        psum = ctx.enter_context(tc.psum_pool(name="psum", bufs=1))
+
+        def sb(name, shape, dtype):
+            return keep.tile(shape, dtype, name=name, align_bytes=64)
+
+        offs_t = sb("offs_t", [P, 32], U16)
+        cand_t = sb("cand_t", [P, 32], U16)
+        nb_t = sb("nb_t", [P, 32], U16)
+        xw = sb("xw", [P, T], I32)
+        xs = sb("xs", [P, T], U8)
+        ww = sb("ww", [P, 2 * S], U8)
+        ws = sb("ws", [P, S], U8)
+        gs_t = sb("gs_t", [P, PACK], F32)
+        warm = sb("warm", [P, 2], F32)
+
+        nc.gpsimd.memset(xs[:].bitcast(I32), 0)
+        nc.gpsimd.memset(ws[:].bitcast(I32), 0)
+        nc.vector.memset(warm[:, 0:1], 0.0)
+        nc.scalar.activation(out=warm[:, 1:2], in_=warm[:, 0:1], func=COPY, scale=0.0625)
+
+        nc.sync.dma_start(offs_t[:], offs)
+        nc.sync.dma_start(ww[:].bitcast(I32), w1_words[0].bitcast(I32))
+        for q in range(4):
+            nc.sync.dma_start(xs[32 * q : 32 * q + 4, :].bitcast(I32), x_scales[0, 4 * q : 4 * q + 4, :].bitcast(I32))
+        nc.sync.dma_start(xw[:], x_words[0].rearrange("p n t -> p (n t)").bitcast(I32))
+        for q in range(4):
+            nc.sync.dma_start(ws[32 * q : 32 * q + 4, :].bitcast(I32), w1_scales[0, 4 * q : 4 * q + 4, :].bitcast(I32))
+        nc.sync.dma_start(cand_t[:], cand)
+        nc.sync.dma_start(nb_t[:], nb)
+        nc.gpsimd.dma_start(gs_t[:], gs.rearrange("(p t) o -> p (t o)", t=PACK))
+
+        wwd = [keep.tile([P, S], U8, name="wwd%d" % a, tag="wwd%d" % a, align_bytes=64) for a in range(2)]
+        wsd = sb("wsd", [P, S], U8)
+        xqw = sb("xqw", [P, S], U32)
+        xqs = sb("xqs", [P, S], U8)
+        xcw = sb("xcw", [P, S], U32)
+        xcsd = sb("xcsd", [P, S], U8)
+
+        for a in range(2):
+            nc.vector.tensor_copy(
+                wwd[a][:].rearrange("p (t m b) -> p t m b", t=2, b=2),
+                ww[:].rearrange("p (m t b) -> p t m b", t=PACK, b=2)[:, 2 * a : 2 * a + 2],
+            )
+        nc.vector.tensor_copy(xqs[:], xs[:].indirect(offs_t[:]))
+        nc.vector.tensor_copy(wsd[:].rearrange("p (t m) -> p t m", t=PACK), ws[:].rearrange("p (m t) -> p t m", t=PACK))
+        nc.vector.tensor_copy(xqw[:], xw[:].bitcast(U32).indirect(offs_t[:]))
+        nc.vector.tensor_copy(xcw[:].rearrange("p (t m) -> p m t", t=PACK), xw[:].bitcast(U32).indirect(cand_t[:]))
+
+        hp = [psum.tile([P, S], F32, name="hp%d" % t) for t in range(PACK)]
+        h = [sb("h%d" % t, [P, S], F32) for t in range(PACK)]
+        gh = [[sb("gh%d_%d" % (t, a), [P, HALF], F32) for a in range(2)] for t in range(PACK)]
+        z32 = [sb("z32_%d" % a, [P, PACK, HALF], F32) for a in range(2)]
+        zb = [sb("zb%d" % c, [P, CH, PACK], BF16) for c in range(NCH)]
+        zw = [sb("zw%d" % c, [P, CH], U32) for c in range(NCH)]
+        zs = [sb("zs%d" % c, [P, CH], U8) for c in range(NCH)]
+        op = [psum.tile([P, PACK, CH], F32, name="op%d" % c) for c in range(NCH)]
+        o32 = [sb("o32_%d" % c, [P, PACK, CH], F32) for c in range(NCH)]
+        ob = [sb("ob%d" % c, [P, CH, PACK], BF16) for c in range(NCH)]
+        ow = [sb("ow%d" % c, [P, CH], I32) for c in range(NCH)]
+        osc = sb("osc", [P, S], U8)
+
+        for t in range(PACK):
+            nc.tensor.matmul_mx(
+                out=hp[t][:],
+                lhsT=wwd[t // 2][:, 256 * (t % 2) : 256 * (t % 2 + 1)].bitcast(FP4X4),
+                lhsT_scale=wsd[:, 128 * t : 128 * (t + 1)],
+                rhs=xqw[:].bitcast(FP8X4),
+                rhs_scale=xqs[:],
+                start=True,
+                stop=True,
+            )
+
+        xcs = keep.tile([P, S], U8, name="xcs", tag="wwd0", align_bytes=64)
+        nc.vector.tensor_copy(xcs[:], xs[:].indirect(cand_t[:]))
+        nc.vector.tensor_copy(xcsd[:].rearrange("p (t m) -> p t m", t=PACK), xcs[:].rearrange("p (m t) -> p t m", t=PACK))
+
+        def scaled(t, a):
+            nc.scalar.activation(out=gh[t][a][:], in_=hp[t][:, HALF * a : HALF * (a + 1)], func=COPY, scale=gs_t[:, t : t + 1])
+
+        def fetch(t, c0, n):
+            a, b = divmod(c0, 2)
+            nc.vector.tensor_tensor(
+                z32[a][:, t, CH * b : CH * (b + n)],
+                h[t][:].indirect(nb_t[:, 8 * c0 : 8 * (c0 + n)]),
+                gh[t][a][:, CH * b : CH * (b + n)],
+                MULT,
+            )
+
+        def weave_z(c, on_scalar):
+            a, b = divmod(c, 2)
+            dst = zb[c][:].rearrange("p (u i) t -> p u t i", i=4)
+            src = z32[a][:, :, CH * b : CH * (b + 1)].rearrange("p t (u i) -> p u t i", i=4)
+            if on_scalar:
+                nc.scalar.copy(dst, src)
+            else:
+                nc.vector.tensor_copy(dst, src)
+
+        def quant_z(c):
+            nc.vector.quantize_mx(out=zw[c][:].bitcast(FP8X4), scales=zs[c][:], in_=zb[c][:].rearrange("p n t -> p (n t)"))
+            for t in range(PACK):
+                nc.tensor.matmul_mx(
+                    out=op[c][:, t, :],
+                    lhsT=xcw[:, 128 * t : 128 * (t + 1)].bitcast(FP8X4),
+                    lhsT_scale=xcsd[:, 128 * t : 128 * (t + 1)],
+                    rhs=zw[c][:].bitcast(FP8X4),
+                    rhs_scale=zs[c][:],
+                    start=True,
+                    stop=True,
+                )
+            nc.scalar.activation(out=o32[c][:], in_=op[c][:], func=COPY, scale=0.0625)
+            nc.sync.dma_start(out_0.rearrange("(p t) j -> p t j", t=PACK)[:, :, CH * c : CH * (c + 1)], o32[c][:])
+
+        def weave_o(c, on_scalar):
+            if on_scalar:
+                nc.scalar.activation(out=ob[c][:], in_=op[c][:].rearrange("p t n -> p n t"), func=COPY, scale=0.0625)
+            else:
+                nc.vector.tensor_copy(
+                    ob[c][:].rearrange("p (u i) t -> p u t i", i=4), o32[c][:].rearrange("p t (u i) -> p u t i", i=4)
+                )
+
+        def quant_o(c):
+            nc.vector.quantize_mx(
+                out=ow[c][:].bitcast(FP8X4), scales=osc[:, CH * c : CH * (c + 1)], in_=ob[c][:].rearrange("p n t -> p (n t)")
+            )
+            nc.sync.dma_start(out_1[0].rearrange("p c r -> p (c r)").bitcast(I32)[:, CH * c : CH * (c + 1)], ow[c][:])
+
+        for t in range(PACK):
+            nc.scalar.activation(out=h[t][:], in_=hp[t][:], func=COPY)
+            scaled(t, 0)
+            fetch(t, 0, 2)
+        for t in range(PACK):
+            scaled(t, 1)
+        weave_z(0, True)
+        weave_z(1, True)
+        for t in range(PACK):
+            fetch(t, 2, 1)
+        quant_z(0)
+        weave_z(2, True)
+        for t in range(PACK):
+            fetch(t, 3, 1)
+        quant_z(1)
+        weave_z(3, False)
+        quant_z(2)
+        quant_z(3)
+        weave_o(0, False)
+        weave_o(1, False)
+        quant_o(0)
+        quant_o(1)
+        weave_o(2, False)
+        quant_o(2)
+        weave_o(3, False)
+        quant_o(3)
+        for q in range(4):
+            eng = nc.scalar if q % 2 else nc.sync
+            eng.dma_start(out_2[0, 4 * q : 4 * q + 4, :].bitcast(I32), osc[32 * q : 32 * q + 4, :].bitcast(I32))

@@ -40,48 +40,66 @@ def tile_picked_candbil_none_po_kernel(
         xw = sb("xw", [P, T], I32)
         xs = sb("xs", [P, T], U8)
         ww = sb("ww", [P, 2 * S], U8)
-        ws = sb("ws", [P, S], U8)
+        ws = keep.tile([P, S], U8, name="ws", tag="ws", align_bytes=64)
         gs_t = sb("gs_t", [P, PACK], F32)
-        warm = sb("warm", [P, 2], F32)
 
-        nc.gpsimd.memset(xs[:].bitcast(I32), 0)
+        def load_xs(eng, q):
+            eng.dma_start(xs[32 * q : 32 * q + 4, :].bitcast(I32), x_scales[0, 4 * q : 4 * q + 4, :].bitcast(I32))
+
+        def load_ws(eng, q):
+            eng.dma_start(ws[32 * q : 32 * q + 4, :].bitcast(I32), w1_scales[0, 4 * q : 4 * q + 4, :].bitcast(I32))
+
+        def load_ww(eng):
+            eng.dma_start(ww[:].bitcast(I32), w1_words[0].bitcast(I32))
+
+        def load_xw(eng):
+            eng.dma_start(xw[:], x_words[0].rearrange("p n t -> p (n t)").bitcast(I32))
+
+        def load_gs(eng):
+            eng.dma_start(gs_t[:], gs.rearrange("(p t) o -> p (t o)", t=PACK))
+
+        nc.gpsimd.memset(xs[:].bitcast(I32)[:, 0:256], 0)
+        nc.vector.memset(xs[:].bitcast(I32)[:, 256:512], 0)
         nc.gpsimd.memset(ws[:].bitcast(I32), 0)
-        nc.vector.memset(warm[:, 0:1], 0.0)
-        nc.scalar.activation(out=warm[:, 1:2], in_=warm[:, 0:1], func=COPY, scale=0.0625)
-
+        load_ww(nc.sync)
         nc.sync.dma_start(offs_t[:], offs)
-        nc.sync.dma_start(ww[:].bitcast(I32), w1_words[0].bitcast(I32))
-        for q in range(4):
-            nc.sync.dma_start(xs[32 * q : 32 * q + 4, :].bitcast(I32), x_scales[0, 4 * q : 4 * q + 4, :].bitcast(I32))
-        nc.sync.dma_start(xw[:], x_words[0].rearrange("p n t -> p (n t)").bitcast(I32))
-        for q in range(4):
-            nc.sync.dma_start(ws[32 * q : 32 * q + 4, :].bitcast(I32), w1_scales[0, 4 * q : 4 * q + 4, :].bitcast(I32))
         nc.sync.dma_start(cand_t[:], cand)
+        for q in range(4):
+            load_xs(nc.sync, q)
+        load_xw(nc.sync)
+        for q in range(4):
+            load_ws(nc.sync, q)
         nc.sync.dma_start(nb_t[:], nb)
-        nc.gpsimd.dma_start(gs_t[:], gs.rearrange("(p t) o -> p (t o)", t=PACK))
+        load_gs(nc.gpsimd)
 
         wwd = [keep.tile([P, S], U8, name="wwd%d" % a, tag="wwd%d" % a, align_bytes=64) for a in range(2)]
         wsd = sb("wsd", [P, S], U8)
         xqw = sb("xqw", [P, S], U32)
         xqs = sb("xqs", [P, S], U8)
-        xcw = sb("xcw", [P, S], U32)
-        xcsd = sb("xcsd", [P, S], U8)
 
-        for a in range(2):
+        def deal_ww(a):
             nc.vector.tensor_copy(
                 wwd[a][:].rearrange("p (t m b) -> p t m b", t=2, b=2),
                 ww[:].rearrange("p (m t b) -> p t m b", t=PACK, b=2)[:, 2 * a : 2 * a + 2],
             )
-        nc.vector.tensor_copy(xqs[:], xs[:].indirect(offs_t[:]))
-        nc.vector.tensor_copy(wsd[:].rearrange("p (t m) -> p t m", t=PACK), ws[:].rearrange("p (m t) -> p t m", t=PACK))
-        nc.vector.tensor_copy(xqw[:], xw[:].bitcast(U32).indirect(offs_t[:]))
-        nc.vector.tensor_copy(xcw[:].rearrange("p (t m) -> p m t", t=PACK), xw[:].bitcast(U32).indirect(cand_t[:]))
+
+        def deal_ws():
+            nc.vector.tensor_copy(wsd[:].rearrange("p (t m) -> p t m", t=PACK), ws[:].rearrange("p (m t) -> p t m", t=PACK))
+
+        def pick_xqs():
+            nc.vector.tensor_copy(xqs[:], xs[:].indirect(offs_t[:]))
+
+        def pick_xqw(a, n):
+            nc.vector.tensor_copy(xqw[:, HALF * a : HALF * (a + n)], xw[:].bitcast(U32).indirect(offs_t[:, 16 * a : 16 * (a + n)]))
+
+        xcs = sb("xcs", [P, S], U8)
 
         hp = [psum.tile([P, S], F32, name="hp%d" % t) for t in range(PACK)]
         h = [sb("h%d" % t, [P, S], F32) for t in range(PACK)]
-        gh = [[sb("gh%d_%d" % (t, a), [P, HALF], F32) for a in range(2)] for t in range(PACK)]
-        z32 = [sb("z32_%d" % a, [P, PACK, HALF], F32) for a in range(2)]
-        zb = [sb("zb%d" % c, [P, CH, PACK], BF16) for c in range(NCH)]
+        gh = [sb("gh%d" % t, [P, S], F32) for t in range(PACK)]
+        z_first = sb("z_first", [P, PACK, HALF], F32)
+        z32 = [z_first[:, :, 0:CH], z_first[:, :, CH:HALF], sb("z32_2", [P, PACK, CH], F32)[:]]
+        zb = [keep.tile([P, CH, PACK], BF16, name="zb%d" % c, tag="zb%d" % c, align_bytes=64) for c in range(NCH)]
         zw = [sb("zw%d" % c, [P, CH], U32) for c in range(NCH)]
         zs = [sb("zs%d" % c, [P, CH], U8) for c in range(NCH)]
         op = [psum.tile([P, PACK, CH], F32, name="op%d" % c) for c in range(NCH)]
@@ -90,37 +108,36 @@ def tile_picked_candbil_none_po_kernel(
         ow = [sb("ow%d" % c, [P, CH], I32) for c in range(NCH)]
         osc = sb("osc", [P, S], U8)
 
-        for t in range(PACK):
+        def project(t, a, n):
+            cols = slice(HALF * a, HALF * (a + n))
             nc.tensor.matmul_mx(
-                out=hp[t][:],
+                out=hp[t][:, cols],
                 lhsT=wwd[t // 2][:, 256 * (t % 2) : 256 * (t % 2 + 1)].bitcast(FP4X4),
                 lhsT_scale=wsd[:, 128 * t : 128 * (t + 1)],
-                rhs=xqw[:].bitcast(FP8X4),
-                rhs_scale=xqs[:],
+                rhs=xqw[:, cols].bitcast(FP8X4),
+                rhs_scale=xqs[:, cols],
                 start=True,
                 stop=True,
             )
 
-        xcs = keep.tile([P, S], U8, name="xcs", tag="wwd0", align_bytes=64)
-        nc.vector.tensor_copy(xcs[:], xs[:].indirect(cand_t[:]))
-        nc.vector.tensor_copy(xcsd[:].rearrange("p (t m) -> p t m", t=PACK), xcs[:].rearrange("p (m t) -> p t m", t=PACK))
+        def window(t):
+            nc.scalar.activation(out=h[t][:], in_=hp[t][:], func=COPY)
 
-        def scaled(t, a):
-            nc.scalar.activation(out=gh[t][a][:], in_=hp[t][:, HALF * a : HALF * (a + 1)], func=COPY, scale=gs_t[:, t : t + 1])
+        def scaled(t, c0, n):
+            cols = slice(CH * c0, CH * (c0 + n))
+            nc.scalar.activation(out=gh[t][:, cols], in_=hp[t][:, cols], func=COPY, scale=gs_t[:, t : t + 1])
+
+        def scaled_v(t):
+            nc.vector.tensor_scalar(gh[t][:, 0:HALF], h[t][:, 0:HALF], gs_t[:, t : t + 1], None, MULT)
 
         def fetch(t, c0, n):
-            a, b = divmod(c0, 2)
-            nc.vector.tensor_tensor(
-                z32[a][:, t, CH * b : CH * (b + n)],
-                h[t][:].indirect(nb_t[:, 8 * c0 : 8 * (c0 + n)]),
-                gh[t][a][:, CH * b : CH * (b + n)],
-                MULT,
-            )
+            cols = slice(CH * c0, CH * (c0 + n))
+            dst = z_first[:, t, :] if n == 2 else z32[c0][:, t, :]
+            nc.vector.tensor_tensor(dst, h[t][:].indirect(nb_t[:, 8 * c0 : 8 * (c0 + n)]), gh[t][:, cols], MULT)
 
         def weave_z(c, on_scalar):
-            a, b = divmod(c, 2)
             dst = zb[c][:].rearrange("p (u i) t -> p u t i", i=4)
-            src = z32[a][:, :, CH * b : CH * (b + 1)].rearrange("p t (u i) -> p u t i", i=4)
+            src = z32[c].rearrange("p t (u i) -> p u t i", i=4)
             if on_scalar:
                 nc.scalar.copy(dst, src)
             else:
@@ -138,6 +155,8 @@ def tile_picked_candbil_none_po_kernel(
                     start=True,
                     stop=True,
                 )
+
+        def out32(c):
             nc.scalar.activation(out=o32[c][:], in_=op[c][:], func=COPY, scale=0.0625)
             nc.sync.dma_start(out_0.rearrange("(p t) j -> p t j", t=PACK)[:, :, CH * c : CH * (c + 1)], o32[c][:])
 
@@ -155,24 +174,44 @@ def tile_picked_candbil_none_po_kernel(
             )
             nc.sync.dma_start(out_1[0].rearrange("p c r -> p (c r)").bitcast(I32)[:, CH * c : CH * (c + 1)], ow[c][:])
 
+        deal_ww(0)
+        deal_ww(1)
+        pick_xqs()
+        deal_ws()
+        pick_xqw(0, 2)
+        nc.vector.tensor_copy(xcs[:], xs[:].indirect(cand_t[:]))
+        xcw = keep.tile([P, S], U32, name="xcw", tag="ws", align_bytes=64)
+        nc.vector.tensor_copy(xcw[:].rearrange("p (t m) -> p m t", t=PACK), xw[:].bitcast(U32).indirect(cand_t[:]))
         for t in range(PACK):
-            nc.scalar.activation(out=h[t][:], in_=hp[t][:], func=COPY)
-            scaled(t, 0)
+            project(t, 0, 2)
+        xcsd = keep.tile([P, S], U8, name="xcsd", tag="wwd0", align_bytes=64)
+        nc.vector.tensor_copy(xcsd[:].rearrange("p (t m) -> p t m", t=PACK), xcs[:].rearrange("p (m t) -> p t m", t=PACK))
+        for t in range(PACK):
+            window(t)
+        scaled_v(0)
+        for t in range(PACK):
+            if t + 1 < PACK:
+                scaled_v(t + 1)
             fetch(t, 0, 2)
         for t in range(PACK):
-            scaled(t, 1)
+            scaled(t, 2, 2)
         weave_z(0, True)
         weave_z(1, True)
         for t in range(PACK):
             fetch(t, 2, 1)
         quant_z(0)
         weave_z(2, True)
+        out32(0)
+        quant_z(1)
+        out32(1)
+        quant_z(2)
+        out32(2)
+        z32.append(keep.tile([P, PACK, CH], F32, name="z32_3", tag="zb0", align_bytes=64)[:])
         for t in range(PACK):
             fetch(t, 3, 1)
-        quant_z(1)
         weave_z(3, False)
-        quant_z(2)
         quant_z(3)
+        out32(3)
         weave_o(0, False)
         weave_o(1, False)
         quant_o(0)
@@ -181,6 +220,7 @@ def tile_picked_candbil_none_po_kernel(
         quant_o(2)
         weave_o(3, False)
         quant_o(3)
+
         for q in range(4):
             eng = nc.scalar if q % 2 else nc.sync
             eng.dma_start(out_2[0, 4 * q : 4 * q + 4, :].bitcast(I32), osc[32 * q : 32 * q + 4, :].bitcast(I32))

@@ -52,8 +52,8 @@ def tile_picked_candbil_none_po_kernel(
         def load_ww(eng):
             eng.dma_start(ww[:].bitcast(I32), w1_words[0].bitcast(I32))
 
-        def load_xw(eng):
-            eng.dma_start(xw[:], x_words[0].rearrange("p n t -> p (n t)").bitcast(I32))
+        def load_xw(a, b):
+            nc.sync.dma_start(xw[:, a:b], x_words[0].rearrange("p n t -> p (n t)").bitcast(I32)[:, a:b])
 
         def load_gs(eng):
             eng.dma_start(gs_t[:], gs.rearrange("(p t) o -> p (t o)", t=PACK))
@@ -63,12 +63,13 @@ def tile_picked_candbil_none_po_kernel(
         nc.gpsimd.memset(ws[:].bitcast(I32), 0)
         load_ww(nc.sync)
         nc.sync.dma_start(offs_t[:], offs)
-        nc.sync.dma_start(cand_t[:], cand)
+        load_xw(0, 512)
         for q in range(4):
             load_xs(nc.sync, q)
-        load_xw(nc.sync)
+        load_xw(512, T)
         for q in range(4):
             load_ws(nc.sync, q)
+        nc.sync.dma_start(cand_t[:], cand)
         nc.sync.dma_start(nb_t[:], nb)
         load_gs(nc.gpsimd)
 
@@ -92,7 +93,6 @@ def tile_picked_candbil_none_po_kernel(
         def pick_xqw(a, n):
             nc.vector.tensor_copy(xqw[:, HALF * a : HALF * (a + n)], xw[:].bitcast(U32).indirect(offs_t[:, 16 * a : 16 * (a + n)]))
 
-        xcs = sb("xcs", [P, S], U8)
 
         hp = [psum.tile([P, S], F32, name="hp%d" % t) for t in range(PACK)]
         h = [sb("h%d" % t, [P, S], F32) for t in range(PACK)]
@@ -103,9 +103,9 @@ def tile_picked_candbil_none_po_kernel(
         zw = [sb("zw%d" % c, [P, CH], U32) for c in range(NCH)]
         zs = [sb("zs%d" % c, [P, CH], U8) for c in range(NCH)]
         op = [psum.tile([P, PACK, CH], F32, name="op%d" % c) for c in range(NCH)]
-        o32 = [sb("o32_%d" % c, [P, PACK, CH], F32) for c in range(NCH)]
-        ob = [sb("ob%d" % c, [P, CH, PACK], BF16) for c in range(NCH)]
-        ow = [sb("ow%d" % c, [P, CH], I32) for c in range(NCH)]
+        o32 = sb("o32", [P, NCH, PACK, CH], F32)
+        ob = sb("ob", [P, S, PACK], BF16)
+        ow = sb("ow", [P, S], I32)
         osc = sb("osc", [P, S], U8)
 
         def project(t, a, n):
@@ -157,41 +157,40 @@ def tile_picked_candbil_none_po_kernel(
                 )
 
         def out32(c):
-            nc.scalar.activation(out=o32[c][:], in_=op[c][:], func=COPY, scale=0.0625)
-            nc.sync.dma_start(out_0.rearrange("(p t) j -> p t j", t=PACK)[:, :, CH * c : CH * (c + 1)], o32[c][:])
+            nc.scalar.activation(out=o32[:, c], in_=op[c][:], func=COPY, scale=0.0625)
+            nc.sync.dma_start(out_0.rearrange("(p t) j -> p t j", t=PACK)[:, :, CH * c : CH * (c + 1)], o32[:, c])
 
-        def weave_o(c, on_scalar):
+        def weave_o(c, n, on_scalar):
+            cols = slice(CH * c, CH * (c + n))
             if on_scalar:
-                nc.scalar.activation(out=ob[c][:], in_=op[c][:].rearrange("p t n -> p n t"), func=COPY, scale=0.0625)
+                nc.scalar.activation(out=ob[:, cols, :], in_=op[c][:].rearrange("p t n -> p n t"), func=COPY, scale=0.0625)
             else:
                 nc.vector.tensor_copy(
-                    ob[c][:].rearrange("p (u i) t -> p u t i", i=4), o32[c][:].rearrange("p t (u i) -> p u t i", i=4)
+                    ob[:, cols, :].rearrange("p (c u i) t -> p c u t i", c=n, i=4),
+                    o32[:, c : c + n].rearrange("p c t (u i) -> p c u t i", i=4),
                 )
 
-        def quant_o(c):
-            nc.vector.quantize_mx(
-                out=ow[c][:].bitcast(FP8X4), scales=osc[:, CH * c : CH * (c + 1)], in_=ob[c][:].rearrange("p n t -> p (n t)")
-            )
-            nc.sync.dma_start(out_1[0].rearrange("p c r -> p (c r)").bitcast(I32)[:, CH * c : CH * (c + 1)], ow[c][:])
+        def quant_o(c, n):
+            cols = slice(CH * c, CH * (c + n))
+            nc.vector.quantize_mx(out=ow[:, cols].bitcast(FP8X4), scales=osc[:, cols], in_=ob[:, cols, :].rearrange("p n t -> p (n t)"))
+            nc.sync.dma_start(out_1[0].rearrange("p c r -> p (c r)").bitcast(I32)[:, cols], ow[:, cols])
 
         deal_ww(0)
         deal_ww(1)
         pick_xqs()
         deal_ws()
         pick_xqw(0, 2)
-        nc.vector.tensor_copy(xcs[:], xs[:].indirect(cand_t[:]))
         xcw = keep.tile([P, S], U32, name="xcw", tag="ws", align_bytes=64)
         nc.vector.tensor_copy(xcw[:].rearrange("p (t m) -> p m t", t=PACK), xw[:].bitcast(U32).indirect(cand_t[:]))
         for t in range(PACK):
             project(t, 0, 2)
-        xcsd = keep.tile([P, S], U8, name="xcsd", tag="wwd0", align_bytes=64)
+        xcs = keep.tile([P, S], U8, name="xcs", tag="wwd0", align_bytes=64)
+        xcsd = sb("xcsd", [P, S], U8)
+        nc.vector.tensor_copy(xcs[:], xs[:].indirect(cand_t[:]))
         nc.vector.tensor_copy(xcsd[:].rearrange("p (t m) -> p t m", t=PACK), xcs[:].rearrange("p (m t) -> p t m", t=PACK))
         for t in range(PACK):
             window(t)
-        scaled_v(0)
-        for t in range(PACK):
-            if t + 1 < PACK:
-                scaled_v(t + 1)
+            scaled(t, 0, 2)
             fetch(t, 0, 2)
         for t in range(PACK):
             scaled(t, 2, 2)
@@ -211,15 +210,13 @@ def tile_picked_candbil_none_po_kernel(
             fetch(t, 3, 1)
         weave_z(3, False)
         quant_z(3)
+        weave_o(3, 1, True)
         out32(3)
-        weave_o(0, False)
-        weave_o(1, False)
-        quant_o(0)
-        quant_o(1)
-        weave_o(2, False)
-        quant_o(2)
-        weave_o(3, False)
-        quant_o(3)
+        weave_o(0, 2, False)
+        weave_o(2, 1, False)
+        quant_o(0, 2)
+        quant_o(2, 1)
+        quant_o(3, 1)
 
         for q in range(4):
             eng = nc.scalar if q % 2 else nc.sync

@@ -173,6 +173,9 @@ def tile_picked_candbil_none_po_kernel(
         def quant_o(c, n):
             cols = slice(CH * c, CH * (c + n))
             nc.vector.quantize_mx(out=ow[:, cols].bitcast(FP8X4), scales=osc[:, cols], in_=ob[:, cols, :].rearrange("p n t -> p (n t)"))
+
+        def store_words(c, n):
+            cols = slice(CH * c, CH * (c + n))
             nc.sync.dma_start(out_1[0].rearrange("p c r -> p (c r)").bitcast(I32)[:, cols], ow[:, cols])
 
         deal_ww(0)
@@ -215,8 +218,10 @@ def tile_picked_candbil_none_po_kernel(
         weave_o(0, 2, False)
         weave_o(2, 1, False)
         quant_o(0, 2)
+        store_words(0, 2)
         quant_o(2, 1)
         quant_o(3, 1)
+        store_words(2, 2)
 
         for q in range(4):
             eng = nc.scalar if q % 2 else nc.sync

@@ -213,15 +213,15 @@ def tile_picked_candbil_none_po_kernel(
             fetch(t, 3, 1)
         weave_z(3, False)
         quant_z(3)
-        weave_o(3, 1, True)
         out32(3)
+        weave_o(3, 1, True)
         weave_o(0, 2, False)
         weave_o(2, 1, False)
         quant_o(0, 2)
-        store_words(0, 2)
         quant_o(2, 1)
+        store_words(0, 3)
         quant_o(3, 1)
-        store_words(2, 2)
+        store_words(3, 1)
 
         for q in range(4):
             eng = nc.scalar if q % 2 else nc.sync

from contextlib import ExitStack

import concourse.mybir as mybir

F32 = mybir.dt.float32
BF16 = mybir.dt.bfloat16
I32 = mybir.dt.int32
U32 = mybir.dt.uint32
U16 = mybir.dt.uint16
U8 = mybir.dt.uint8
FP8X4 = mybir.dt.float8_e4m3fn_x4
FP4X4 = mybir.dt.float4_e2m1fn_x4
COPY = mybir.ActivationFunctionType.Copy
MULT = mybir.AluOpType.mult

P = 128
T = 2048
S = 512
PACK = 4
CH = 128
NCH = S // CH
HALF = 256
FLOPS = 2 * 2 * 512 * 512 * 512


def tile_picked_candbil_none_po_kernel(
    tc, x_words, x_scales, w1_words, w1_scales, gs, offs, nb, cand, out_0, out_1, out_2
):
    nc = tc.nc
    with ExitStack() as ctx:
        keep = ctx.enter_context(tc.tile_pool(name="keep", bufs=1))
        psum = ctx.enter_context(tc.psum_pool(name="psum", bufs=1))

        def sb(name, shape, dtype):
            return keep.tile(shape, dtype, name=name, align_bytes=64)

        offs_t = sb("offs_t", [P, 32], U16)
        cand_t = sb("cand_t", [P, 32], U16)
        nb_t = sb("nb_t", [P, 32], U16)
        xw = sb("xw", [P, T], I32)
        xs = sb("xs", [P, T], U8)
        ww = sb("ww", [P, 2 * S], U8)
        ws = keep.tile([P, S], U8, name="ws", tag="ws", align_bytes=64)
        gs_t = sb("gs_t", [P, PACK], F32)

        def load_xs(eng, q):
            eng.dma_start(xs[32 * q : 32 * q + 4, :].bitcast(I32), x_scales[0, 4 * q : 4 * q + 4, :].bitcast(I32))

        def load_ws(eng, q):
            eng.dma_start(ws[32 * q : 32 * q + 4, :].bitcast(I32), w1_scales[0, 4 * q : 4 * q + 4, :].bitcast(I32))

        def load_ww(eng):
            eng.dma_start(ww[:].bitcast(I32), w1_words[0].bitcast(I32))

        def load_xw(a, b):
            nc.sync.dma_start(xw[:, a:b], x_words[0].rearrange("p n t -> p (n t)").bitcast(I32)[:, a:b])

        def load_gs(eng):
            eng.dma_start(gs_t[:], gs.rearrange("(p t) o -> p (t o)", t=PACK))

        nc.gpsimd.memset(xs[:].bitcast(I32)[:, 0:256], 0)
        nc.vector.memset(xs[:].bitcast(I32)[:, 256:512], 0)
        nc.gpsimd.memset(ws[:].bitcast(I32), 0)
        load_ww(nc.sync)
        nc.sync.dma_start(offs_t[:], offs)
        load_xw(0, 512)
        for q in range(4):
            load_xs(nc.sync, q)
        load_xw(512, T)
        for q in range(4):
            load_ws(nc.sync, q)
        nc.sync.dma_start(cand_t[:], cand)
        nc.sync.dma_start(nb_t[:], nb)
        load_gs(nc.gpsimd)

        wwd = [keep.tile([P, S], U8, name="wwd%d" % a, tag="wwd%d" % a, align_bytes=64) for a in range(2)]
        wsd = sb("wsd", [P, S], U8)
        xqw = sb("xqw", [P, S], U32)
        xqs = sb("xqs", [P, S], U8)

        def deal_ww(a):
            nc.vector.tensor_copy(
                wwd[a][:].rearrange("p (t m b) -> p t m b", t=2, b=2),
                ww[:].rearrange("p (m t b) -> p t m b", t=PACK, b=2)[:, 2 * a : 2 * a + 2],
            )

        def deal_ws():
            nc.vector.tensor_copy(wsd[:].rearrange("p (t m) -> p t m", t=PACK), ws[:].rearrange("p (m t) -> p t m", t=PACK))

        def pick_xqs():
            nc.vector.tensor_copy(xqs[:], xs[:].indirect(offs_t[:]))

        def pick_xqw(a, n):
            nc.vector.tensor_copy(xqw[:, HALF * a : HALF * (a + n)], xw[:].bitcast(U32).indirect(offs_t[:, 16 * a : 16 * (a + n)]))


        hp = [psum.tile([P, S], F32, name="hp%d" % t) for t in range(PACK)]
        h = [sb("h%d" % t, [P, S], F32) for t in range(PACK)]
        gh = [sb("gh%d" % t, [P, S], F32) for t in range(PACK)]
        z_first = sb("z_first", [P, PACK, HALF], F32)
        z32 = [z_first[:, :, 0:CH], z_first[:, :, CH:HALF], sb("z32_2", [P, PACK, CH], F32)[:]]
        zb = [keep.tile([P, CH, PACK], BF16, name="zb%d" % c, tag="zb%d" % c, align_bytes=64) for c in range(NCH)]
        zw = [sb("zw%d" % c, [P, CH], U32) for c in range(NCH)]
        zs = [sb("zs%d" % c, [P, CH], U8) for c in range(NCH)]
        op = [psum.tile([P, PACK, CH], F32, name="op%d" % c) for c in range(NCH)]
        o32 = sb("o32", [P, NCH, PACK, CH], F32)
        ob = sb("ob", [P, S, PACK], BF16)
        ow = sb("ow", [P, S], I32)
        osc = sb("osc", [P, S], U8)

        def project(t, a, n):
            cols = slice(HALF * a, HALF * (a + n))
            nc.tensor.matmul_mx(
                out=hp[t][:, cols],
                lhsT=wwd[t // 2][:, 256 * (t % 2) : 256 * (t % 2 + 1)].bitcast(FP4X4),
                lhsT_scale=wsd[:, 128 * t : 128 * (t + 1)],
                rhs=xqw[:, cols].bitcast(FP8X4),
                rhs_scale=xqs[:, cols],
                start=True,
                stop=True,
            )

        def window(t):
            nc.scalar.activation(out=h[t][:], in_=hp[t][:], func=COPY)

        def scaled(t, c0, n):
            cols = slice(CH * c0, CH * (c0 + n))
            nc.scalar.activation(out=gh[t][:, cols], in_=hp[t][:, cols], func=COPY, scale=gs_t[:, t : t + 1])

        def scaled_v(t):
            nc.vector.tensor_scalar(gh[t][:, 0:HALF], h[t][:, 0:HALF], gs_t[:, t : t + 1], None, MULT)

        def fetch(t, c0, n):
            cols = slice(CH * c0, CH * (c0 + n))
            dst = z_first[:, t, :] if n == 2 else z32[c0][:, t, :]
            nc.vector.tensor_tensor(dst, h[t][:].indirect(nb_t[:, 8 * c0 : 8 * (c0 + n)]), gh[t][:, cols], MULT)

        def weave_z(c, on_scalar):
            dst = zb[c][:].rearrange("p (u i) t -> p u t i", i=4)
            src = z32[c].rearrange("p t (u i) -> p u t i", i=4)
            if on_scalar:
                nc.scalar.copy(dst, src)
            else:
                nc.vector.tensor_copy(dst, src)

        def quant_z(c):
            nc.vector.quantize_mx(out=zw[c][:].bitcast(FP8X4), scales=zs[c][:], in_=zb[c][:].rearrange("p n t -> p (n t)"))
            for t in range(PACK):
                nc.tensor.matmul_mx(
                    out=op[c][:, t, :],
                    lhsT=xcw[:, 128 * t : 128 * (t + 1)].bitcast(FP8X4),
                    lhsT_scale=xcsd[:, 128 * t : 128 * (t + 1)],
                    rhs=zw[c][:].bitcast(FP8X4),
                    rhs_scale=zs[c][:],
                    start=True,
                    stop=True,
                )

        def out32(c):
            nc.scalar.activation(out=o32[:, c], in_=op[c][:], func=COPY, scale=0.0625)
            nc.sync.dma_start(out_0.rearrange("(p t) j -> p t j", t=PACK)[:, :, CH * c : CH * (c + 1)], o32[:, c])

        def weave_o(c, n, on_scalar):
            cols = slice(CH * c, CH * (c + n))
            if on_scalar:
                nc.scalar.activation(out=ob[:, cols, :], in_=op[c][:].rearrange("p t n -> p n t"), func=COPY, scale=0.0625)
            else:
                nc.vector.tensor_copy(
                    ob[:, cols, :].rearrange("p (c u i) t -> p c u t i", c=n, i=4),
                    o32[:, c : c + n].rearrange("p c t (u i) -> p c u t i", i=4),
                )

        def quant_o(c, n):
            cols = slice(CH * c, CH * (c + n))
            nc.vector.quantize_mx(out=ow[:, cols].bitcast(FP8X4), scales=osc[:, cols], in_=ob[:, cols, :].rearrange("p n t -> p (n t)"))

        def store_words(c, n):
            cols = slice(CH * c, CH * (c + n))
            nc.sync.dma_start(out_1[0].rearrange("p c r -> p (c r)").bitcast(I32)[:, cols], ow[:, cols])

        deal_ww(0)
        deal_ww(1)
        pick_xqs()
        deal_ws()
        pick_xqw(0, 2)
        xcw = keep.tile([P, S], U32, name="xcw", tag="ws", align_bytes=64)
        nc.vector.tensor_copy(xcw[:].rearrange("p (t m) -> p m t", t=PACK), xw[:].bitcast(U32).indirect(cand_t[:]))
        for t in range(PACK):
            project(t, 0, 2)
        xcs = keep.tile([P, S], U8, name="xcs", tag="wwd0", align_bytes=64)
        xcsd = sb("xcsd", [P, S], U8)
        nc.vector.tensor_copy(xcs[:], xs[:].indirect(cand_t[:]))
        nc.vector.tensor_copy(xcsd[:].rearrange("p (t m) -> p t m", t=PACK), xcs[:].rearrange("p (m t) -> p t m", t=PACK))
        for t in range(PACK):
            window(t)
            scaled(t, 0, 2)
            fetch(t, 0, 2)
        for t in range(PACK):
            scaled(t, 2, 2)
        weave_z(0, True)
        weave_z(1, True)
        for t in range(PACK):
            fetch(t, 2, 1)
        quant_z(0)
        weave_z(2, True)
        out32(0)
        quant_z(1)
        out32(1)
        quant_z(2)
        out32(2)
        z32.append(keep.tile([P, PACK, CH], F32, name="z32_3", tag="zb0", align_bytes=64)[:])
        for t in range(PACK):
            fetch(t, 3, 1)
        weave_z(3, False)
        quant_z(3)
        out32(3)
        weave_o(3, 1, True)
        weave_o(0, 2, False)
        weave_o(2, 1, False)
        quant_o(0, 2)
        quant_o(2, 1)
        store_words(0, 3)
        quant_o(3, 1)
        store_words(3, 1)

        for q in range(4):
            eng = nc.scalar if q % 2 else nc.sync
            eng.dma_start(out_2[0, 4 * q : 4 * q + 4, :].bitcast(I32), osc[32 * q : 32 * q + 4, :].bitcast(I32))
